import numpy as np
import ml_dtypes


def mxq(x, axis, fmt="e4m3"):
    dtype, down = {"e4m3": (ml_dtypes.float8_e4m3fn, 7), "e5m2": (ml_dtypes.float8_e5m2, 14)}[fmt]
    v = np.moveaxis(np.asarray(x, np.float32).astype(ml_dtypes.bfloat16).astype(np.float64), axis, -1)
    blocks = v.reshape(v.shape[:-1] + (-1, 32))
    amax = np.abs(blocks).max(-1, keepdims=True)
    byte = np.maximum(np.where(amax > 0, np.frexp(amax)[1] - 1 + 127, 0) - down, 1)
    scale = np.exp2(byte - 127.0)
    codes = (blocks / scale).astype(np.float32).astype(dtype).astype(np.float64)
    return np.moveaxis((codes * scale).reshape(v.shape), -1, axis)


WIDE = False


def mx_kscale(k):
    if not WIDE:
        return np.ones(k)
    levels = np.array([10, -10, 5, -5, 0])
    if k % 512:
        return np.exp2(np.random.permutation(np.resize(levels, k // 32))).repeat(32)
    a = np.empty((k // 512, 16))
    for p in range(k // 512):
        a[p, :8] = np.random.permutation(np.resize(levels, 8))
        for g in range(8):
            far = levels[np.abs(levels - a[p, g]) >= 10]
            a[p, g + 8] = far[np.random.randint(len(far))]
    return np.exp2(a.ravel()).repeat(32)


def f64(x):
    return np.asarray(x).astype(np.float64)


def striped(idx):
    return np.tile(idx.reshape(-1, 16).T, (8, 1)).astype(np.uint16)


def unstriped(offs):
    return offs[:16].T.reshape(-1).astype(np.int64)


def striped8(idx):
    return np.concatenate([x.reshape(-1, 16).T for x in idx]).astype(np.uint16)


def runs(offs, k):
    lists = np.stack([offs[16 * r : 16 * r + 16].T.reshape(-1) for r in range(8)]).astype(np.int64)
    return lists[np.arange(k) % 512 // 64]


def pack_weight(w):
    k, n = w.shape
    w = f64(np.asarray(w, np.float32).astype(ml_dtypes.bfloat16)).reshape(k // 32, 32, n)
    amax = np.abs(w).max(1)
    byte = np.clip(np.where(amax > 0, np.frexp(amax)[1] - 1 + 127 - 7, 1), 1, 254)
    scaled = (w * np.exp2(127.0 - byte)[:, None, :]).reshape(k, n).astype(np.float32)
    words = np.ascontiguousarray(scaled.reshape(k // 512, 128, 4, n).transpose(0, 1, 3, 2)).astype(ml_dtypes.float8_e4m3fn).view(np.uint8)
    return words, np.ascontiguousarray(byte.astype(np.uint8).reshape(k // 512, 16, n))


def unpack_weight(words, scales):
    g, p, n, _ = words.shape
    vals = np.ascontiguousarray(words).view(ml_dtypes.float8_e4m3fn).astype(np.float64) * np.repeat(np.exp2(scales.astype(np.float64) - 127.0), 8, axis=1)[..., None]
    return vals.transpose(0, 1, 3, 2).reshape(g * 512, n)


K, T, S, G, H, J = 512, 1024, 512, 2048, 512, 512


def setup_inputs():
    n = np.random.standard_normal
    s = mx_kscale(K)[:, None]
    packed_xT = pack_weight(n((K, T)) * s)
    packed_dT = pack_weight(n((K, G)) / s)
    return {
        "x_words": packed_xT[0],
        "x_scales": packed_xT[1],
        "d_words": packed_dT[0],
        "d_scales": packed_dT[1],
        "gs": (np.random.uniform(0.5, 1.5, (K, 1)) * s).astype(np.float32),
        "tab": n((H, J)).astype(np.float32),
        "offs": striped(np.random.permutation(T)[:S]),
        "k1": striped8(np.random.randint(0, G, (8, H))),
        "n1": striped8(np.stack([np.random.permutation(S) for _ in range(8)])),
        "n2": striped8(np.stack([np.random.permutation(S) for _ in range(8)])),
        "k2": striped8(np.random.randint(0, G, (8, H))),
        "n3": striped8(np.random.randint(0, J, (8, S))),
        "n4": striped8(np.stack([np.random.permutation(S) for _ in range(8)])),
    }


def reference(x_words, x_scales, d_words, d_scales, gs, tab, offs, k1, n1, n2, k2, n3, n4):
    d_k2 = unpack_weight(d_words, d_scales)[np.arange(K)[:, None], runs(k2, K)]
    d_k1 = unpack_weight(d_words, d_scales)[np.arange(K)[:, None], runs(k1, K)]
    xq = unpack_weight(x_words, x_scales)[:, unstriped(offs)]
    h = 0.0625 * (d_k1.T @ xq)
    z = f64(gs) * ((h[np.arange(H)[:, None], runs(n1, H)]) * (h[np.arange(H)[:, None], runs(n2, H)]))
    h2 = 0.0625 * ((d_k2.T @ mxq(z, 0, "e4m3")))
    return np.abs(h2 - (h2[np.arange(H)[:, None], runs(n4, H)]) - (f64(tab)[np.arange(H)[:, None], runs(n3, H)]))

@@ -1,0 +1,184 @@
+from contextlib import ExitStack
+
+import concourse.mybir as mybir
+
+K, T, S, G, H, J = 512, 1024, 512, 2048, 512, 512
+FLOPS = 2 * K * H * S + 2 * H * H * S
+
+F32 = mybir.dt.float32
+BF16 = mybir.dt.bfloat16
+I32 = mybir.dt.int32
+U32 = mybir.dt.uint32
+U16 = mybir.dt.uint16
+U8 = mybir.dt.uint8
+FP8X4 = mybir.dt.float8_e4m3fn_x4
+ALU = mybir.AluOpType
+ACT = mybir.ActivationFunctionType
+
+P = 128
+PACK = 4
+HALF = S // 2
+LIST_COLS = HALF // 16
+
+
+def tile_picked_codeprodkindd_none_p_kernel(tc, x_words, x_scales, d_words, d_scales, gs, tab, offs, k1, n1, n2, k2, n3, n4, out):
+    nc = tc.nc
+    with ExitStack() as ctx:
+        lists = ctx.enter_context(tc.tile_pool(name="lists", bufs=1))
+        pool = ctx.enter_context(tc.tile_pool(name="sbuf", bufs=1))
+        psum = ctx.enter_context(tc.psum_pool(name="psum", bufs=1))
+
+        def sb(name, shape, dtype, tag=None):
+            return pool.tile(shape, dtype, name=name, tag=tag or name, align_bytes=64)
+
+        def load_list(name, src):
+            tile = lists.tile([P, S // 16], U16, name=name)
+            nc.sync.dma_start(tile[:], src)
+            return tile
+
+        def half_of(lst, c):
+            return lst[:, c * LIST_COLS : (c + 1) * LIST_COLS]
+
+        def cols(c):
+            return slice(c * HALF, (c + 1) * HALF)
+
+        xs_win = sb("xs_win", [P, T], U8)
+        ds_win = sb("ds_win", [P, G], U8)
+        nc.vector.memset(ds_win[:].bitcast(I32), 0)
+        nc.vector.memset(xs_win[:].bitcast(I32), 0)
+        k1_t = load_list("k1_t", k1)
+        nc.scalar.dma_start(ds_win[0:P:8, :].bitcast(I32), d_scales[0].bitcast(I32))
+        offs_t = load_list("offs_t", offs)
+        nc.scalar.dma_start(xs_win[0:P:8, :].bitcast(I32), x_scales[0].bitcast(I32))
+        xw_win = sb("xw_win", [P, T], U32)
+        dw_win = sb("dw_win", [P, G], U32)
+        nc.sync.dma_start(dw_win[:].bitcast(I32), d_words[0].rearrange("p n t -> p (n t)").bitcast(I32))
+        nc.sync.dma_start(xw_win[:].bitcast(I32), x_words[0].rearrange("p n t -> p (n t)").bitcast(I32))
+        gs_t = sb("gs_t", [P, PACK], F32)
+        nc.sync.dma_start(gs_t[:], gs.rearrange("(p t) o -> p (t o)", t=PACK))
+        k2_t = load_list("k2_t", k2)
+        n1_t = load_list("n1_t", n1)
+        n2_t = load_list("n2_t", n2)
+        n3_t = load_list("n3_t", n3)
+        n4_t = load_list("n4_t", n4)
+
+        x_plane = sb("x_plane", [P, S], U8)
+        w1_plane = sb("w1_plane", [P, H], U8)
+        w2_plane = sb("w2_plane", [P, H], U8)
+        for plane in (x_plane, w1_plane, w2_plane):
+            nc.vector.memset(plane[:].bitcast(I32), 0)
+        gain = sb("gain", [P, PACK], F32)
+        nc.scalar.activation(gain[:], gs_t[:], ACT.Copy, scale=0.0625 * 0.0625)
+
+        def place_rows(queue, plane, src):
+            for i in range(PACK):
+                queue.dma_start(plane[i:P:32, :].bitcast(I32), src[8 * i : P : 32, :].bitcast(I32))
+
+        def deal(dst, src):
+            nc.vector.tensor_copy(dst[:].rearrange("p (t m) -> p m t", t=PACK), src[:].rearrange("p (m t) -> p m t", t=PACK))
+
+        def pick(name, win, lst, dtype, tag=None):
+            got = sb(name, [P, S], dtype, tag=tag)
+            nc.vector.tensor_copy(got[:], win[:].indirect(lst[:]))
+            return got
+
+        s1_got = pick("s1_got", ds_win, k1_t, U8)
+        xs_got = pick("xs_got", xs_win, offs_t, U8)
+        s1_dealt = sb("s1_dealt", [P, H], U8)
+        deal(s1_dealt, s1_got)
+        place_rows(nc.scalar, x_plane, xs_got)
+        place_rows(nc.scalar, w1_plane, s1_dealt)
+
+        w1_got = pick("w1_got", dw_win, k1_t, U32)
+        x_got = pick("x_got", xw_win, offs_t, U32)
+        w1 = sb("w1", [P, H], U32)
+        deal(w1, w1_got)
+        s2_got = pick("s2_got", ds_win, k2_t, U8, tag="xw_win")
+        w2_got = pick("w2_got", dw_win, k2_t, U32, tag="w1_got")
+        s2_dealt = sb("s2_dealt", [P, H], U8)
+        deal(s2_dealt, s2_got)
+        place_rows(nc.sync, w2_plane, s2_dealt)
+        w2 = sb("w2", [P, H], U32)
+        deal(w2, w2_got)
+
+        tab_rows = tab.rearrange("(p t) j -> t p j", t=PACK)
+        out_rows = out.rearrange("(p t) j -> t p j", t=PACK)
+        tab_win = []
+        for t, tag in enumerate(("s1_dealt", "ds_win", "dw_win", "w1_got")):
+            win = sb(f"tab{t}", [P, J], F32, tag=tag)
+            nc.sync.dma_start(win[:], tab_rows[t])
+            tab_win.append(win)
+
+        h = []
+        for t in range(PACK):
+            m_cols = slice(t * P, (t + 1) * P)
+            acc = psum.tile([P, S], F32, name=f"acc1_{t}", tag=f"bank{t}")
+            nc.tensor.matmul_mx(
+                out=acc[:], lhsT=w1[:, m_cols].bitcast(FP8X4), lhsT_scale=w1_plane[:, m_cols],
+                rhs=x_got[:].bitcast(FP8X4), rhs_scale=x_plane[:], start=True, stop=True,
+            )
+            win = sb(f"h{t}", [P, S], F32)
+            nc.scalar.copy(win[:], acc[:])
+            h.append(win)
+
+        h2 = [sb(f"h2_{t}", [P, S], F32) for t in range(PACK)]
+        z = [sb(f"z{c}", [P, HALF, PACK], BF16) for c in range(2)]
+
+        def first_factor(c, t, dst):
+            nc.vector.tensor_copy(dst, h[t][:].indirect(half_of(n1_t, c)))
+
+        def product(c, t, first):
+            prod = sb(f"prod{c}{t}", [P, HALF], F32)
+            nc.vector.tensor_tensor(prod[:], h[t][:].indirect(half_of(n2_t, c)), first, ALU.mult)
+            nc.scalar.activation(z[c][:, :, t], prod[:], ACT.Copy, scale=gain[:, t : t + 1])
+
+        def pair_products(c, t0, tag=None):
+            first = sb(f"first{c}{t0}", [P, 2, HALF], F32, tag=tag)
+            for i in range(2):
+                first_factor(c, t0 + i, first[:, i, :])
+            for i in range(2):
+                product(c, t0 + i, first[:, i, :])
+
+        def second_layer(c):
+            codes = sb(f"zc{c}", [P, HALF], U32)
+            plane = sb(f"zs{c}", [P, HALF], U8)
+            nc.vector.quantize_mx(out=codes[:].bitcast(FP8X4), scales=plane[:], in_=z[c][:].rearrange("p j t -> p (j t)"))
+            for t in range(PACK):
+                m_cols = slice(t * P, (t + 1) * P)
+                acc = psum.tile([P, HALF], F32, name=f"acc2_{c}{t}", tag=f"bank{(1 - c) * PACK + t}")
+                nc.tensor.matmul_mx(
+                    out=acc[:], lhsT=w2[:, m_cols].bitcast(FP8X4), lhsT_scale=w2_plane[:, m_cols],
+                    rhs=codes[:].bitcast(FP8X4), rhs_scale=plane[:], start=True, stop=True,
+                )
+                nc.scalar.activation(h2[t][:, cols(c)], acc[:], ACT.Copy, scale=0.0625)
+
+        def kind_less_h2(c, t, dst):
+            nc.vector.tensor_tensor(dst, tab_win[t][:].indirect(half_of(n3_t, c)), h2[t][:, cols(c)], ALU.subtract)
+
+        def finish(c, t, part):
+            total = sb(f"total{c}{t}", [P, HALF], F32)
+            nc.vector.tensor_tensor(total[:], h2[t][:].indirect(half_of(n4_t, c)), part, ALU.add)
+            res = sb(f"res{c}{t}", [P, HALF], F32)
+            nc.scalar.activation(res[:], total[:], ACT.Abs)
+            nc.sync.dma_start(out_rows[t][:, cols(c)], res[:])
+
+        pair_products(0, 0)
+        pair_products(0, 2)
+        pair_products(1, 0)
+        second_layer(0)
+        pair_products(1, 2, tag="prod03")
+        second_layer(1)
+        part = {}
+        for t0, tag in ((0, None), (2, "prod13")):
+            both = sb(f"part0{t0}", [P, 2, HALF], F32, tag=tag)
+            for i in range(2):
+                part[0, t0 + i] = both[:, i, :]
+                kind_less_h2(0, t0 + i, part[0, t0 + i])
+        for t in range(PACK):
+            finish(0, t, part[0, t])
+            late = sb(f"part1{t}", [P, HALF], F32)
+            part[1, t] = late[:]
+            kind_less_h2(1, t, part[1, t])
+            if t > 0:
+                finish(1, t - 1, part[1, t - 1])
+        finish(1, PACK - 1, part[1, PACK - 1])

@@ -42,95 +42,106 @@ def tile_picked_codeprodkindd_none_p_kernel(tc, x_words, x_scales, d_words, d_sc
         def cols(c):
             return slice(c * HALF, (c + 1) * HALF)
 
-        xs_win = sb("xs_win", [P, T], U8)
-        ds_win = sb("ds_win", [P, G], U8)
-        nc.vector.memset(ds_win[:].bitcast(I32), 0)
-        nc.vector.memset(xs_win[:].bitcast(I32), 0)
-        k1_t = load_list("k1_t", k1)
-        nc.scalar.dma_start(ds_win[0:P:8, :].bitcast(I32), d_scales[0].bitcast(I32))
+        def load_scale_rows(name, src, width):
+            win = sb(name, [P, width], U8)
+            rows = src[0].bitcast(I32)
+            nc.sync.dma_start(win[:].bitcast(I32), rows.unsqueeze(1).to_broadcast([16, 8, width // 4]))
+            return win
+
+        def load_words(name, src, width):
+            win = sb(name, [P, width], U32)
+            nc.sync.dma_start(win[:].bitcast(I32), src[0].rearrange("p n t -> p (n t)").bitcast(I32))
+            return win
+
         offs_t = load_list("offs_t", offs)
-        nc.scalar.dma_start(xs_win[0:P:8, :].bitcast(I32), x_scales[0].bitcast(I32))
-        xw_win = sb("xw_win", [P, T], U32)
-        dw_win = sb("dw_win", [P, G], U32)
-        nc.sync.dma_start(dw_win[:].bitcast(I32), d_words[0].rearrange("p n t -> p (n t)").bitcast(I32))
-        nc.sync.dma_start(xw_win[:].bitcast(I32), x_words[0].rearrange("p n t -> p (n t)").bitcast(I32))
-        gs_t = sb("gs_t", [P, PACK], F32)
-        nc.sync.dma_start(gs_t[:], gs.rearrange("(p t) o -> p (t o)", t=PACK))
+        xs_win = load_scale_rows("xs_win", x_scales, T)
+        k1_t = load_list("k1_t", k1)
+        ds_win = load_scale_rows("ds_win", d_scales, G)
         k2_t = load_list("k2_t", k2)
+        xw_win = load_words("xw_win", x_words, T)
+        dw_win = load_words("dw_win", d_words, G)
         n1_t = load_list("n1_t", n1)
         n2_t = load_list("n2_t", n2)
         n3_t = load_list("n3_t", n3)
         n4_t = load_list("n4_t", n4)
+        gs_t = sb("gs_t", [P, PACK], F32)
+        nc.gpsimd.dma_start(gs_t[:], gs.rearrange("(p t) o -> p (t o)", t=PACK))
 
-        x_plane = sb("x_plane", [P, S], U8)
-        w1_plane = sb("w1_plane", [P, H], U8)
-        w2_plane = sb("w2_plane", [P, H], U8)
-        for plane in (x_plane, w1_plane, w2_plane):
-            nc.vector.memset(plane[:].bitcast(I32), 0)
         gain = sb("gain", [P, PACK], F32)
         nc.scalar.activation(gain[:], gs_t[:], ACT.Copy, scale=0.0625 * 0.0625)
 
-        def place_rows(queue, plane, src):
-            for i in range(PACK):
-                queue.dma_start(plane[i:P:32, :].bitcast(I32), src[8 * i : P : 32, :].bitcast(I32))
-
-        def deal(dst, src):
-            nc.vector.tensor_copy(dst[:].rearrange("p (t m) -> p m t", t=PACK), src[:].rearrange("p (m t) -> p m t", t=PACK))
+        def deal(dst, src, run):
+            nc.vector.tensor_copy(
+                dst.rearrange("p (c t b i) -> p c b t i", c=dst.shape[1] // H, t=PACK, i=run),
+                src.rearrange("p (c b i t) -> p c b t i", c=dst.shape[1] // H, t=PACK, i=run),
+            )
 
         def pick(name, win, lst, dtype, tag=None):
             got = sb(name, [P, S], dtype, tag=tag)
             nc.vector.tensor_copy(got[:], win[:].indirect(lst[:]))
             return got
 
-        s1_got = pick("s1_got", ds_win, k1_t, U8)
         xs_got = pick("xs_got", xs_win, offs_t, U8)
-        s1_dealt = sb("s1_dealt", [P, H], U8)
-        deal(s1_dealt, s1_got)
-        place_rows(nc.scalar, x_plane, xs_got)
-        place_rows(nc.scalar, w1_plane, s1_dealt)
+        ds_got = sb("ds_got", [P, 2 * H], U8)
+        nc.vector.tensor_copy(ds_got[:, 0:H], ds_win[:].indirect(k1_t[:]))
+        nc.vector.tensor_copy(ds_got[:, H : 2 * H], ds_win[:].indirect(k2_t[:]))
+        planes = sb("planes", [P, 2 * H + S], U8)
+        nc.vector.tensor_copy(planes[:, 2 * H :].bitcast(I32), xs_got[:].bitcast(I32))
+        deal(planes[:, 0 : 2 * H], ds_got[:], 16)
+        for i in range(1, PACK):
+            nc.scalar.dma_start(planes[i:P:32, :].bitcast(I32), planes[8 * i : P : 32, :].bitcast(I32))
 
-        w1_got = pick("w1_got", dw_win, k1_t, U32)
         x_got = pick("x_got", xw_win, offs_t, U32)
+        w1_got = pick("w1_got", dw_win, k1_t, U32)
         w1 = sb("w1", [P, H], U32)
-        deal(w1, w1_got)
-        s2_got = pick("s2_got", ds_win, k2_t, U8, tag="xw_win")
+        deal(w1[:], w1_got[:], 4)
         w2_got = pick("w2_got", dw_win, k2_t, U32, tag="w1_got")
-        s2_dealt = sb("s2_dealt", [P, H], U8)
-        deal(s2_dealt, s2_got)
-        place_rows(nc.sync, w2_plane, s2_dealt)
         w2 = sb("w2", [P, H], U32)
-        deal(w2, w2_got)
+        deal(w2[:], w2_got[:], 4)
 
         tab_rows = tab.rearrange("(p t) j -> t p j", t=PACK)
         out_rows = out.rearrange("(p t) j -> t p j", t=PACK)
-        tab_win = []
-        for t, tag in enumerate(("s1_dealt", "ds_win", "dw_win", "w1_got")):
-            win = sb(f"tab{t}", [P, J], F32, tag=tag)
-            nc.sync.dma_start(win[:], tab_rows[t])
-            tab_win.append(win)
-
-        h = []
+        h, gh, accs = [], [], []
         for t in range(PACK):
             m_cols = slice(t * P, (t + 1) * P)
             acc = psum.tile([P, S], F32, name=f"acc1_{t}", tag=f"bank{t}")
             nc.tensor.matmul_mx(
-                out=acc[:], lhsT=w1[:, m_cols].bitcast(FP8X4), lhsT_scale=w1_plane[:, m_cols],
-                rhs=x_got[:].bitcast(FP8X4), rhs_scale=x_plane[:], start=True, stop=True,
+                out=acc[:], lhsT=w1[:, m_cols].bitcast(FP8X4), lhsT_scale=planes[:, m_cols],
+                rhs=x_got[:].bitcast(FP8X4), rhs_scale=planes[:, 2 * H :], start=True, stop=True,
             )
-            win = sb(f"h{t}", [P, S], F32)
-            nc.scalar.copy(win[:], acc[:])
-            h.append(win)
+            accs.append(acc)
+        for t0 in range(0, PACK, 2):
+            for t in (t0, t0 + 1):
+                win = sb(f"gh{t}", [P, S], F32)
+                nc.scalar.activation(win[:], accs[t][:], ACT.Copy, scale=gain[:, t : t + 1])
+                gh.append(win)
+            for t in (t0, t0 + 1):
+                win = sb(f"h{t}", [P, S], F32)
+                nc.scalar.copy(win[:], accs[t][:])
+                h.append(win)
+
+        tab_win = []
+        for t, tag in enumerate(("dw_win", "w1_got", "x_got", "w1")):
+            win = sb(f"tab{t}", [P, J], F32, tag=tag)
+            nc.sync.dma_start(win[:], tab_rows[t])
+            tab_win.append(win)
 
         h2 = [sb(f"h2_{t}", [P, S], F32) for t in range(PACK)]
         z = [sb(f"z{c}", [P, HALF, PACK], BF16) for c in range(2)]
 
+        prod = [sb(f"prod{c}", [P, PACK, HALF], F32) for c in range(2)]
+
         def first_factor(c, t, dst):
-            nc.vector.tensor_copy(dst, h[t][:].indirect(half_of(n1_t, c)))
+            nc.vector.tensor_copy(dst, gh[t][:].indirect(half_of(n1_t, c)))
 
         def product(c, t, first):
-            prod = sb(f"prod{c}{t}", [P, HALF], F32)
-            nc.vector.tensor_tensor(prod[:], h[t][:].indirect(half_of(n2_t, c)), first, ALU.mult)
-            nc.scalar.activation(z[c][:, :, t], prod[:], ACT.Copy, scale=gain[:, t : t + 1])
+            nc.vector.tensor_tensor(prod[c][:, t, :], h[t][:].indirect(half_of(n2_t, c)), first, ALU.mult)
+
+        def interleave(c):
+            nc.scalar.copy(
+                z[c][:].rearrange("p (b i) t -> p b t i", i=4),
+                prod[c][:].rearrange("p t (b i) -> p b t i", i=4),
+            )
 
         def pair_products(c, t0, tag=None):
             first = sb(f"first{c}{t0}", [P, 2, HALF], F32, tag=tag)
@@ -147,7 +158,7 @@ def tile_picked_codeprodkindd_none_p_kernel(tc, x_words, x_scales, d_words, d_sc
                 m_cols = slice(t * P, (t + 1) * P)
                 acc = psum.tile([P, HALF], F32, name=f"acc2_{c}{t}", tag=f"bank{(1 - c) * PACK + t}")
                 nc.tensor.matmul_mx(
-                    out=acc[:], lhsT=w2[:, m_cols].bitcast(FP8X4), lhsT_scale=w2_plane[:, m_cols],
+                    out=acc[:], lhsT=w2[:, m_cols].bitcast(FP8X4), lhsT_scale=planes[:, H + t * P : H + (t + 1) * P],
                     rhs=codes[:].bitcast(FP8X4), rhs_scale=plane[:], start=True, stop=True,
                 )
                 nc.scalar.activation(h2[t][:, cols(c)], acc[:], ACT.Copy, scale=0.0625)
@@ -164,12 +175,14 @@ def tile_picked_codeprodkindd_none_p_kernel(tc, x_words, x_scales, d_words, d_sc
 
         pair_products(0, 0)
         pair_products(0, 2)
+        interleave(0)
         pair_products(1, 0)
         second_layer(0)
-        pair_products(1, 2, tag="prod03")
+        pair_products(1, 2, tag="prod0")
+        interleave(1)
         second_layer(1)
         part = {}
-        for t0, tag in ((0, None), (2, "prod13")):
+        for t0, tag in ((0, None), (2, "prod1")):
             both = sb(f"part0{t0}", [P, 2, HALF], F32, tag=tag)
             for i in range(2):
                 part[0, t0 + i] = both[:, i, :]

@@ -18,7 +18,8 @@ ACT = mybir.ActivationFunctionType
 P = 128
 PACK = 4
 HALF = S // 2
-LIST_COLS = HALF // 16
+LINE = 16
+SIXTEENTH = 0.0625
 
 
 def tile_picked_codeprodkindd_none_p_kernel(tc, x_words, x_scales, d_words, d_scales, gs, tab, offs, k1, n1, n2, k2, n3, n4, out):
@@ -26,6 +27,7 @@ def tile_picked_codeprodkindd_none_p_kernel(tc, x_words, x_scales, d_words, d_sc
     with ExitStack() as ctx:
         lists = ctx.enter_context(tc.tile_pool(name="lists", bufs=1))
         pool = ctx.enter_context(tc.tile_pool(name="sbuf", bufs=1))
+        picked = ctx.enter_context(tc.tile_pool(name="picked", bufs=1))
         psum = ctx.enter_context(tc.psum_pool(name="psum", bufs=1))
 
         def sb(name, shape, dtype, tag=None):
@@ -35,12 +37,6 @@ def tile_picked_codeprodkindd_none_p_kernel(tc, x_words, x_scales, d_words, d_sc
             tile = lists.tile([P, S // 16], U16, name=name)
             nc.sync.dma_start(tile[:], src)
             return tile
-
-        def half_of(lst, c):
-            return lst[:, c * LIST_COLS : (c + 1) * LIST_COLS]
-
-        def cols(c):
-            return slice(c * HALF, (c + 1) * HALF)
 
         def load_scale_rows(name, src, width):
             win = sb(name, [P, width], U8)
@@ -53,6 +49,16 @@ def tile_picked_codeprodkindd_none_p_kernel(tc, x_words, x_scales, d_words, d_sc
             nc.sync.dma_start(win[:].bitcast(I32), src[0].rearrange("p n t -> p (n t)").bitcast(I32))
             return win
 
+        def entries(lst, j0, j1):
+            return lst[:, j0 // 16 : j1 // 16]
+
+        def wide_window(name):
+            win = sb(name, [P, 2 * S], F32)
+            nc.vector.memset(win[:, S:], 0.0)
+            return win
+
+        gs_t = sb("gs_t", [P, PACK], F32)
+        nc.scalar.dma_start(gs_t[:], gs.rearrange("(p t) o -> p (t o)", t=PACK))
         offs_t = load_list("offs_t", offs)
         xs_win = load_scale_rows("xs_win", x_scales, T)
         k1_t = load_list("k1_t", k1)
@@ -64,78 +70,84 @@ def tile_picked_codeprodkindd_none_p_kernel(tc, x_words, x_scales, d_words, d_sc
         n2_t = load_list("n2_t", n2)
         n3_t = load_list("n3_t", n3)
         n4_t = load_list("n4_t", n4)
-        gs_t = sb("gs_t", [P, PACK], F32)
-        nc.gpsimd.dma_start(gs_t[:], gs.rearrange("(p t) o -> p (t o)", t=PACK))
 
         gain = sb("gain", [P, PACK], F32)
-        nc.scalar.activation(gain[:], gs_t[:], ACT.Copy, scale=0.0625 * 0.0625)
+        nc.scalar.activation(gain[:], gs_t[:], ACT.Copy, scale=SIXTEENTH * SIXTEENTH)
+        gh = [wide_window("gh0"), sb("gh1", [P, S], F32), sb("gh2", [P, S], F32), sb("gh3", [P, S], F32)]
+        h2 = [wide_window("h2_0"), wide_window("h2_1"), wide_window("h2_2"), sb("h2_3", [P, S], F32)]
+
+        def pick(got, win, lst):
+            nc.vector.tensor_copy(got[:], win[:].indirect(lst[:]))
 
         def deal(dst, src, run):
             nc.vector.tensor_copy(
-                dst.rearrange("p (c t b i) -> p c b t i", c=dst.shape[1] // H, t=PACK, i=run),
-                src.rearrange("p (c b i t) -> p c b t i", c=dst.shape[1] // H, t=PACK, i=run),
+                dst.rearrange("p (t b i) -> p b t i", t=PACK, i=run),
+                src.rearrange("p (b i t) -> p b t i", t=PACK, i=run),
             )
 
-        def pick(name, win, lst, dtype, tag=None):
-            got = sb(name, [P, S], dtype, tag=tag)
-            nc.vector.tensor_copy(got[:], win[:].indirect(lst[:]))
-            return got
+        def place_scale_rows(plane):
+            for i in range(1, PACK):
+                nc.scalar.dma_start(plane[i:P:32, :].bitcast(I32), plane[8 * i : P : 32, :].bitcast(I32))
 
-        xs_got = pick("xs_got", xs_win, offs_t, U8)
-        ds_got = sb("ds_got", [P, 2 * H], U8)
-        nc.vector.tensor_copy(ds_got[:, 0:H], ds_win[:].indirect(k1_t[:]))
-        nc.vector.tensor_copy(ds_got[:, H : 2 * H], ds_win[:].indirect(k2_t[:]))
-        planes = sb("planes", [P, 2 * H + S], U8)
-        nc.vector.tensor_copy(planes[:, 2 * H :].bitcast(I32), xs_got[:].bitcast(I32))
-        deal(planes[:, 0 : 2 * H], ds_got[:], 16)
-        for i in range(1, PACK):
-            nc.scalar.dma_start(planes[i:P:32, :].bitcast(I32), planes[8 * i : P : 32, :].bitcast(I32))
+        xs_got = sb("xs_got", [P, S], U8)
+        s1_got = sb("s1_got", [P, H], U8)
+        pick(xs_got, xs_win, offs_t)
+        pick(s1_got, ds_win, k1_t)
+        planes1 = sb("planes1", [P, H + S], U8)
+        nc.vector.tensor_copy(planes1[:, H:].bitcast(I32), xs_got[:].bitcast(I32))
+        deal(planes1[:, :H], s1_got[:], LINE)
+        place_scale_rows(planes1)
 
-        x_got = pick("x_got", xw_win, offs_t, U32)
-        w1_got = pick("w1_got", dw_win, k1_t, U32)
+        x_got = sb("x_got", [P, S], U32)
+        w1_got = picked.tile([P, H], U32, name="w1_got", offset=0, align_bytes=64)
+        pick(x_got, xw_win, offs_t)
+        pick(w1_got, dw_win, k1_t)
         w1 = sb("w1", [P, H], U32)
-        deal(w1[:], w1_got[:], 4)
-        w2_got = pick("w2_got", dw_win, k2_t, U32, tag="w1_got")
-        w2 = sb("w2", [P, H], U32)
-        deal(w2[:], w2_got[:], 4)
+        deal(w1[:], w1_got[:], LINE // 4)
 
-        tab_rows = tab.rearrange("(p t) j -> t p j", t=PACK)
-        out_rows = out.rearrange("(p t) j -> t p j", t=PACK)
-        h, gh, accs = [], [], []
+        s2_got = picked.tile([P, H], U8, name="s2_got", offset=0, align_bytes=64)
+        w2_got = picked.tile([P, H], U32, name="w2_got", offset=H, align_bytes=64)
+        pick(s2_got, ds_win, k2_t)
+        pick(w2_got, dw_win, k2_t)
+        plane2 = sb("plane2", [P, H], U8)
+        deal(plane2[:], s2_got[:], LINE)
+        place_scale_rows(plane2)
+        w2 = sb("w2", [P, H], U32)
+        deal(w2[:], w2_got[:], LINE // 4)
+
+        accs = []
         for t in range(PACK):
             m_cols = slice(t * P, (t + 1) * P)
             acc = psum.tile([P, S], F32, name=f"acc1_{t}", tag=f"bank{t}")
             nc.tensor.matmul_mx(
-                out=acc[:], lhsT=w1[:, m_cols].bitcast(FP8X4), lhsT_scale=planes[:, m_cols],
-                rhs=x_got[:].bitcast(FP8X4), rhs_scale=planes[:, 2 * H :], start=True, stop=True,
+                out=acc[:], lhsT=w1[:, m_cols].bitcast(FP8X4), lhsT_scale=planes1[:, m_cols],
+                rhs=x_got[:].bitcast(FP8X4), rhs_scale=planes1[:, H:], start=True, stop=True,
             )
             accs.append(acc)
+        h = [sb(f"h{t}", [P, S], F32) for t in range(PACK)]
         for t0 in range(0, PACK, 2):
             for t in (t0, t0 + 1):
-                win = sb(f"gh{t}", [P, S], F32)
-                nc.scalar.activation(win[:], accs[t][:], ACT.Copy, scale=gain[:, t : t + 1])
-                gh.append(win)
+                nc.scalar.activation(gh[t][:, :S], accs[t][:], ACT.Copy, scale=gain[:, t : t + 1])
             for t in (t0, t0 + 1):
-                win = sb(f"h{t}", [P, S], F32)
-                nc.scalar.copy(win[:], accs[t][:])
-                h.append(win)
+                nc.scalar.copy(h[t][:], accs[t][:])
 
+        tab_rows = tab.rearrange("(p t) j -> t p j", t=PACK)
+        out_rows = out.rearrange("(p t) j -> t p j", t=PACK)
         tab_win = []
-        for t, tag in enumerate(("dw_win", "w1_got", "x_got", "w1")):
+        for t, tag in enumerate(("ds_win", "dw_win", "x_got", "w1")):
             win = sb(f"tab{t}", [P, J], F32, tag=tag)
             nc.sync.dma_start(win[:], tab_rows[t])
             tab_win.append(win)
 
-        h2 = [sb(f"h2_{t}", [P, S], F32) for t in range(PACK)]
         z = [sb(f"z{c}", [P, HALF, PACK], BF16) for c in range(2)]
+        prod = []
 
-        prod = [sb(f"prod{c}", [P, PACK, HALF], F32) for c in range(2)]
+        def first_factor(dst, t, j0, j1):
+            nc.vector.tensor_copy(dst, gh[t][:].indirect(entries(n1_t, j0, j1)))
 
-        def first_factor(c, t, dst):
-            nc.vector.tensor_copy(dst, gh[t][:].indirect(half_of(n1_t, c)))
-
-        def product(c, t, first):
-            nc.vector.tensor_tensor(prod[c][:, t, :], h[t][:].indirect(half_of(n2_t, c)), first, ALU.mult)
+        def product(c, t):
+            window = h[t][:].indirect(entries(n2_t, c * HALF, (c + 1) * HALF))
+            nc.vector.tensor_tensor(prod[c][:, t, :], window, first[c, t], ALU.mult)
 
         def interleave(c):
             nc.scalar.copy(
@@ -143,55 +155,62 @@ def tile_picked_codeprodkindd_none_p_kernel(tc, x_words, x_scales, d_words, d_sc
                 prod[c][:].rearrange("p t (b i) -> p b t i", i=4),
             )
 
-        def pair_products(c, t0, tag=None):
-            first = sb(f"first{c}{t0}", [P, 2, HALF], F32, tag=tag)
-            for i in range(2):
-                first_factor(c, t0 + i, first[:, i, :])
-            for i in range(2):
-                product(c, t0 + i, first[:, i, :])
-
         def second_layer(c):
-            codes = sb(f"zc{c}", [P, HALF], U32)
-            plane = sb(f"zs{c}", [P, HALF], U8)
+            codes = sb(f"z_codes{c}", [P, HALF], U32)
+            plane = sb(f"z_plane{c}", [P, HALF], U8)
             nc.vector.quantize_mx(out=codes[:].bitcast(FP8X4), scales=plane[:], in_=z[c][:].rearrange("p j t -> p (j t)"))
             for t in range(PACK):
                 m_cols = slice(t * P, (t + 1) * P)
                 acc = psum.tile([P, HALF], F32, name=f"acc2_{c}{t}", tag=f"bank{(1 - c) * PACK + t}")
                 nc.tensor.matmul_mx(
-                    out=acc[:], lhsT=w2[:, m_cols].bitcast(FP8X4), lhsT_scale=planes[:, H + t * P : H + (t + 1) * P],
+                    out=acc[:], lhsT=w2[:, m_cols].bitcast(FP8X4), lhsT_scale=plane2[:, m_cols],
                     rhs=codes[:].bitcast(FP8X4), rhs_scale=plane[:], start=True, stop=True,
                 )
-                nc.scalar.activation(h2[t][:, cols(c)], acc[:], ACT.Copy, scale=0.0625)
+                nc.scalar.activation(h2[t][:, c * HALF : (c + 1) * HALF], acc[:], ACT.Copy, scale=SIXTEENTH)
 
-        def kind_less_h2(c, t, dst):
-            nc.vector.tensor_tensor(dst, tab_win[t][:].indirect(half_of(n3_t, c)), h2[t][:, cols(c)], ALU.subtract)
-
-        def finish(c, t, part):
-            total = sb(f"total{c}{t}", [P, HALF], F32)
-            nc.vector.tensor_tensor(total[:], h2[t][:].indirect(half_of(n4_t, c)), part, ALU.add)
-            res = sb(f"res{c}{t}", [P, HALF], F32)
-            nc.scalar.activation(res[:], total[:], ACT.Abs)
-            nc.sync.dma_start(out_rows[t][:, cols(c)], res[:])
-
-        pair_products(0, 0)
-        pair_products(0, 2)
+        first = {}
+        whole = sb("first0", [P, S], F32)
+        first[0, 0], first[1, 0] = whole[:, :HALF], whole[:, HALF:]
+        for t in range(1, PACK):
+            first[0, t] = sb(f"first_a{t}", [P, HALF], F32)[:]
+        prod.append(sb("prod0", [P, PACK, HALF], F32, tag="prod"))
+        for t0 in range(0, PACK, 2):
+            for t in (t0, t0 + 1):
+                first_factor(whole[:] if t == 0 else first[0, t], t, 0, S if t == 0 else HALF)
+            for t in (t0, t0 + 1):
+                product(0, t)
         interleave(0)
-        pair_products(1, 0)
+        late = sb("first_b", [P, PACK - 1, HALF], F32, tag="first_a2")
+        for t in range(1, PACK):
+            first[1, t] = late[:, t - 1, :]
+            first_factor(first[1, t], t, HALF, S)
         second_layer(0)
-        pair_products(1, 2, tag="prod0")
+        prod.append(sb("prod1", [P, PACK, HALF], F32, tag="prod"))
+        for t in range(PACK):
+            product(1, t)
         interleave(1)
         second_layer(1)
-        part = {}
-        for t0, tag in ((0, None), (2, "prod1")):
-            both = sb(f"part0{t0}", [P, 2, HALF], F32, tag=tag)
-            for i in range(2):
-                part[0, t0 + i] = both[:, i, :]
-                kind_less_h2(0, t0 + i, part[0, t0 + i])
+
+        def kind_less_h2(c, t):
+            j0, j1 = c * HALF, (c + 1) * HALF
+            nc.vector.tensor_tensor(part[t][:, j0:j1], tab_win[t][:].indirect(entries(n3_t, j0, j1)), h2[t][:, j0:j1], ALU.subtract)
+
+        def finish(t, j0, j1):
+            total = sb(f"total{t}_{j0}", [P, j1 - j0], F32)
+            nc.vector.tensor_tensor(total[:], h2[t][:].indirect(entries(n4_t, j0, j1)), part[t][:, j0:j1], ALU.add)
+            res = sb(f"res{t}_{j0}", [P, j1 - j0], F32)
+            nc.scalar.activation(res[:], total[:], ACT.Abs)
+            nc.sync.dma_start(out_rows[t][:, j0:j1], res[:])
+
+        part_low = sb("part_low", [P, 2, S], F32)
+        part_high = sb("part_high", [P, 2, S], F32, tag="prod")
+        part = [part_low[:, 0, :], part_low[:, 1, :], part_high[:, 0, :], part_high[:, 1, :]]
         for t in range(PACK):
-            finish(0, t, part[0, t])
-            late = sb(f"part1{t}", [P, HALF], F32)
-            part[1, t] = late[:]
-            kind_less_h2(1, t, part[1, t])
-            if t > 0:
-                finish(1, t - 1, part[1, t - 1])
-        finish(1, PACK - 1, part[1, PACK - 1])
+            kind_less_h2(0, t)
+        kind_less_h2(1, 0)
+        for t in range(PACK - 1):
+            kind_less_h2(1, t + 1)
+            finish(t, 0, S)
+        finish(PACK - 1, 0, HALF)
+        finish(PACK - 1, HALF, HALF + P)
+        finish(PACK - 1, HALF + P, S)

@@ -38,10 +38,10 @@ def tile_picked_codeprodkindd_none_p_kernel(tc, x_words, x_scales, d_words, d_sc
             nc.sync.dma_start(tile[:], src)
             return tile
 
-        def load_scale_rows(name, src, width):
+        def load_scale_rows(queue, name, src, width):
             win = sb(name, [P, width], U8)
             rows = src[0].bitcast(I32)
-            nc.sync.dma_start(win[:].bitcast(I32), rows.unsqueeze(1).to_broadcast([16, 8, width // 4]))
+            queue.dma_start(win[:].bitcast(I32), rows.unsqueeze(1).to_broadcast([16, 8, width // 4]))
             return win
 
         def load_words(name, src, width):
@@ -57,12 +57,12 @@ def tile_picked_codeprodkindd_none_p_kernel(tc, x_words, x_scales, d_words, d_sc
             nc.vector.memset(win[:, S:], 0.0)
             return win
 
+        offs_t = load_list("offs_t", offs)
+        xs_win = load_scale_rows(nc.scalar, "xs_win", x_scales, T)
+        k1_t = load_list("k1_t", k1)
         gs_t = sb("gs_t", [P, PACK], F32)
         nc.scalar.dma_start(gs_t[:], gs.rearrange("(p t) o -> p (t o)", t=PACK))
-        offs_t = load_list("offs_t", offs)
-        xs_win = load_scale_rows("xs_win", x_scales, T)
-        k1_t = load_list("k1_t", k1)
-        ds_win = load_scale_rows("ds_win", d_scales, G)
+        ds_win = load_scale_rows(nc.sync, "ds_win", d_scales, G)
         k2_t = load_list("k2_t", k2)
         xw_win = load_words("xw_win", x_words, T)
         dw_win = load_words("dw_win", d_words, G)
@@ -151,8 +151,8 @@ def tile_picked_codeprodkindd_none_p_kernel(tc, x_words, x_scales, d_words, d_sc
 
         def interleave(c):
             nc.scalar.copy(
-                z[c][:].rearrange("p (b i) t -> p b t i", i=4),
-                prod[c][:].rearrange("p t (b i) -> p b t i", i=4),
+                z[c][:].rearrange("p (b i) t -> p b t i", i=2),
+                prod[c][:].rearrange("p t (b i) -> p b t i", i=2),
             )
 
         def second_layer(c):

@@ -85,6 +85,12 @@ def tile_picked_codeprodkindd_none_p_kernel(tc, x_words, x_scales, d_words, d_sc
                 src.rearrange("p (b i t) -> p b t i", t=PACK, i=run),
             )
 
+        def deal_words(dst, src):
+            nc.vector.tensor_copy(
+                dst.rearrange("p (u v b i) -> p b u i v", u=2, v=2, i=LINE // 4),
+                src.rearrange("p (b i u v) -> p b u i v", u=2, v=2, i=LINE // 4),
+            )
+
         def place_scale_rows(plane):
             for i in range(1, PACK):
                 nc.scalar.dma_start(plane[i:P:32, :].bitcast(I32), plane[8 * i : P : 32, :].bitcast(I32))
@@ -103,7 +109,7 @@ def tile_picked_codeprodkindd_none_p_kernel(tc, x_words, x_scales, d_words, d_sc
         pick(x_got, xw_win, offs_t)
         pick(w1_got, dw_win, k1_t)
         w1 = sb("w1", [P, H], U32)
-        deal(w1[:], w1_got[:], LINE // 4)
+        deal_words(w1[:], w1_got[:])
 
         s2_got = picked.tile([P, H], U8, name="s2_got", offset=0, align_bytes=64)
         w2_got = picked.tile([P, H], U32, name="w2_got", offset=H, align_bytes=64)
@@ -113,7 +119,7 @@ def tile_picked_codeprodkindd_none_p_kernel(tc, x_words, x_scales, d_words, d_sc
         deal(plane2[:], s2_got[:], LINE)
         place_scale_rows(plane2)
         w2 = sb("w2", [P, H], U32)
-        deal(w2[:], w2_got[:], LINE // 4)
+        deal_words(w2[:], w2_got[:])
 
         accs = []
         for t in range(PACK):

from contextlib import ExitStack

import concourse.mybir as mybir

K, T, S, G, H, J = 512, 1024, 512, 2048, 512, 512
FLOPS = 2 * K * H * S + 2 * H * H * S

F32 = mybir.dt.float32
BF16 = mybir.dt.bfloat16
I32 = mybir.dt.int32
U32 = mybir.dt.uint32
U16 = mybir.dt.uint16
U8 = mybir.dt.uint8
FP8X4 = mybir.dt.float8_e4m3fn_x4
ALU = mybir.AluOpType
ACT = mybir.ActivationFunctionType

P = 128
PACK = 4
HALF = S // 2
LINE = 16
SIXTEENTH = 0.0625


def tile_picked_codeprodkindd_none_p_kernel(tc, x_words, x_scales, d_words, d_scales, gs, tab, offs, k1, n1, n2, k2, n3, n4, out):
    nc = tc.nc
    with ExitStack() as ctx:
        lists = ctx.enter_context(tc.tile_pool(name="lists", bufs=1))
        pool = ctx.enter_context(tc.tile_pool(name="sbuf", bufs=1))
        picked = ctx.enter_context(tc.tile_pool(name="picked", bufs=1))
        psum = ctx.enter_context(tc.psum_pool(name="psum", bufs=1))

        def sb(name, shape, dtype, tag=None):
            return pool.tile(shape, dtype, name=name, tag=tag or name, align_bytes=64)

        def load_list(name, src):
            tile = lists.tile([P, S // 16], U16, name=name)
            nc.sync.dma_start(tile[:], src)
            return tile

        def load_scale_rows(queue, name, src, width):
            win = sb(name, [P, width], U8)
            rows = src[0].bitcast(I32)
            queue.dma_start(win[:].bitcast(I32), rows.unsqueeze(1).to_broadcast([16, 8, width // 4]))
            return win

        def load_words(name, src, width):
            win = sb(name, [P, width], U32)
            nc.sync.dma_start(win[:].bitcast(I32), src[0].rearrange("p n t -> p (n t)").bitcast(I32))
            return win

        def entries(lst, j0, j1):
            return lst[:, j0 // 16 : j1 // 16]

        def wide_window(name):
            win = sb(name, [P, 2 * S], F32)
            nc.vector.memset(win[:, S:], 0.0)
            return win

        offs_t = load_list("offs_t", offs)
        xs_win = load_scale_rows(nc.scalar, "xs_win", x_scales, T)
        k1_t = load_list("k1_t", k1)
        gs_t = sb("gs_t", [P, PACK], F32)
        nc.scalar.dma_start(gs_t[:], gs.rearrange("(p t) o -> p (t o)", t=PACK))
        ds_win = load_scale_rows(nc.sync, "ds_win", d_scales, G)
        k2_t = load_list("k2_t", k2)
        xw_win = load_words("xw_win", x_words, T)
        dw_win = load_words("dw_win", d_words, G)
        n1_t = load_list("n1_t", n1)
        n2_t = load_list("n2_t", n2)
        n3_t = load_list("n3_t", n3)
        n4_t = load_list("n4_t", n4)

        gain = sb("gain", [P, PACK], F32)
        nc.scalar.activation(gain[:], gs_t[:], ACT.Copy, scale=SIXTEENTH * SIXTEENTH)
        gh = [wide_window("gh0"), sb("gh1", [P, S], F32), sb("gh2", [P, S], F32), sb("gh3", [P, S], F32)]
        h2 = [wide_window("h2_0"), wide_window("h2_1"), wide_window("h2_2"), sb("h2_3", [P, S], F32)]

        def pick(got, win, lst):
            nc.vector.tensor_copy(got[:], win[:].indirect(lst[:]))

        def deal(dst, src, run):
            nc.vector.tensor_copy(
                dst.rearrange("p (t b i) -> p b t i", t=PACK, i=run),
                src.rearrange("p (b i t) -> p b t i", t=PACK, i=run),
            )

        def deal_words(dst, src):
            nc.vector.tensor_copy(
                dst.rearrange("p (u v b i) -> p b u i v", u=2, v=2, i=LINE // 4),
                src.rearrange("p (b i u v) -> p b u i v", u=2, v=2, i=LINE // 4),
            )

        def place_scale_rows(plane):
            for i in range(1, PACK):
                nc.scalar.dma_start(plane[i:P:32, :].bitcast(I32), plane[8 * i : P : 32, :].bitcast(I32))

        xs_got = sb("xs_got", [P, S], U8)
        s1_got = sb("s1_got", [P, H], U8)
        pick(xs_got, xs_win, offs_t)
        pick(s1_got, ds_win, k1_t)
        planes1 = sb("planes1", [P, H + S], U8)
        nc.vector.tensor_copy(planes1[:, H:].bitcast(I32), xs_got[:].bitcast(I32))
        deal(planes1[:, :H], s1_got[:], LINE)
        place_scale_rows(planes1)

        x_got = sb("x_got", [P, S], U32)
        w1_got = picked.tile([P, H], U32, name="w1_got", offset=0, align_bytes=64)
        pick(x_got, xw_win, offs_t)
        pick(w1_got, dw_win, k1_t)
        w1 = sb("w1", [P, H], U32)
        deal_words(w1[:], w1_got[:])

        s2_got = picked.tile([P, H], U8, name="s2_got", offset=0, align_bytes=64)
        w2_got = picked.tile([P, H], U32, name="w2_got", offset=H, align_bytes=64)
        pick(s2_got, ds_win, k2_t)
        pick(w2_got, dw_win, k2_t)
        plane2 = sb("plane2", [P, H], U8)
        deal(plane2[:], s2_got[:], LINE)
        place_scale_rows(plane2)
        w2 = sb("w2", [P, H], U32)
        deal_words(w2[:], w2_got[:])

        accs = []
        for t in range(PACK):
            m_cols = slice(t * P, (t + 1) * P)
            acc = psum.tile([P, S], F32, name=f"acc1_{t}", tag=f"bank{t}")
            nc.tensor.matmul_mx(
                out=acc[:], lhsT=w1[:, m_cols].bitcast(FP8X4), lhsT_scale=planes1[:, m_cols],
                rhs=x_got[:].bitcast(FP8X4), rhs_scale=planes1[:, H:], start=True, stop=True,
            )
            accs.append(acc)
        h = [sb(f"h{t}", [P, S], F32) for t in range(PACK)]
        for t0 in range(0, PACK, 2):
            for t in (t0, t0 + 1):
                nc.scalar.activation(gh[t][:, :S], accs[t][:], ACT.Copy, scale=gain[:, t : t + 1])
            for t in (t0, t0 + 1):
                nc.scalar.copy(h[t][:], accs[t][:])

        tab_rows = tab.rearrange("(p t) j -> t p j", t=PACK)
        out_rows = out.rearrange("(p t) j -> t p j", t=PACK)
        tab_win = []
        for t, tag in enumerate(("ds_win", "dw_win", "x_got", "w1")):
            win = sb(f"tab{t}", [P, J], F32, tag=tag)
            nc.sync.dma_start(win[:], tab_rows[t])
            tab_win.append(win)

        z = [sb(f"z{c}", [P, HALF, PACK], BF16) for c in range(2)]
        prod = []

        def first_factor(dst, t, j0, j1):
            nc.vector.tensor_copy(dst, gh[t][:].indirect(entries(n1_t, j0, j1)))

        def product(c, t):
            window = h[t][:].indirect(entries(n2_t, c * HALF, (c + 1) * HALF))
            nc.vector.tensor_tensor(prod[c][:, t, :], window, first[c, t], ALU.mult)

        def interleave(c):
            nc.scalar.copy(
                z[c][:].rearrange("p (b i) t -> p b t i", i=2),
                prod[c][:].rearrange("p t (b i) -> p b t i", i=2),
            )

        def second_layer(c):
            codes = sb(f"z_codes{c}", [P, HALF], U32)
            plane = sb(f"z_plane{c}", [P, HALF], U8)
            nc.vector.quantize_mx(out=codes[:].bitcast(FP8X4), scales=plane[:], in_=z[c][:].rearrange("p j t -> p (j t)"))
            for t in range(PACK):
                m_cols = slice(t * P, (t + 1) * P)
                acc = psum.tile([P, HALF], F32, name=f"acc2_{c}{t}", tag=f"bank{(1 - c) * PACK + t}")
                nc.tensor.matmul_mx(
                    out=acc[:], lhsT=w2[:, m_cols].bitcast(FP8X4), lhsT_scale=plane2[:, m_cols],
                    rhs=codes[:].bitcast(FP8X4), rhs_scale=plane[:], start=True, stop=True,
                )
                nc.scalar.activation(h2[t][:, c * HALF : (c + 1) * HALF], acc[:], ACT.Copy, scale=SIXTEENTH)

        first = {}
        whole = sb("first0", [P, S], F32)
        first[0, 0], first[1, 0] = whole[:, :HALF], whole[:, HALF:]
        for t in range(1, PACK):
            first[0, t] = sb(f"first_a{t}", [P, HALF], F32)[:]
        prod.append(sb("prod0", [P, PACK, HALF], F32, tag="prod"))
        for t0 in range(0, PACK, 2):
            for t in (t0, t0 + 1):
                first_factor(whole[:] if t == 0 else first[0, t], t, 0, S if t == 0 else HALF)
            for t in (t0, t0 + 1):
                product(0, t)
        interleave(0)
        late = sb("first_b", [P, PACK - 1, HALF], F32, tag="first_a2")
        for t in range(1, PACK):
            first[1, t] = late[:, t - 1, :]
            first_factor(first[1, t], t, HALF, S)
        second_layer(0)
        prod.append(sb("prod1", [P, PACK, HALF], F32, tag="prod"))
        for t in range(PACK):
            product(1, t)
        interleave(1)
        second_layer(1)

        def kind_less_h2(c, t):
            j0, j1 = c * HALF, (c + 1) * HALF
            nc.vector.tensor_tensor(part[t][:, j0:j1], tab_win[t][:].indirect(entries(n3_t, j0, j1)), h2[t][:, j0:j1], ALU.subtract)

        def finish(t, j0, j1):
            total = sb(f"total{t}_{j0}", [P, j1 - j0], F32)
            nc.vector.tensor_tensor(total[:], h2[t][:].indirect(entries(n4_t, j0, j1)), part[t][:, j0:j1], ALU.add)
            res = sb(f"res{t}_{j0}", [P, j1 - j0], F32)
            nc.scalar.activation(res[:], total[:], ACT.Abs)
            nc.sync.dma_start(out_rows[t][:, j0:j1], res[:])

        part_low = sb("part_low", [P, 2, S], F32)
        part_high = sb("part_high", [P, 2, S], F32, tag="prod")
        part = [part_low[:, 0, :], part_low[:, 1, :], part_high[:, 0, :], part_high[:, 1, :]]
        for t in range(PACK):
            kind_less_h2(0, t)
        kind_less_h2(1, 0)
        for t in range(PACK - 1):
            kind_less_h2(1, t + 1)
            finish(t, 0, S)
        finish(PACK - 1, 0, HALF)
        finish(PACK - 1, HALF, HALF + P)
        finish(PACK - 1, HALF + P, S)
